import numpy as np, ml_dtypes
CORES = [73,201,329,457,330]
N = 5
W, KW, DIL = 1024, 3, 4
H = (KW // 2) * DIL
def setup_inputs(rng):
    return {"x": rng.standard_normal((N, 128, W), dtype=np.float32).astype(ml_dtypes.bfloat16), "w": rng.standard_normal((N, 128, KW * 128), dtype=np.float32).astype(ml_dtypes.bfloat16)}
def setup_inputs_big(rng):
    d = setup_inputs(rng)
    for k in ("x", "w"): d[k] = (d[k].astype(np.float32) * 1024.0).astype(d[k].dtype)
    return d
def setup_inputs_small(rng):
    d = setup_inputs(rng)
    for k in ("x", "w"): d[k] = (d[k].astype(np.float32) * (1 / 1024.0)).astype(d[k].dtype)
    return d
def reference(x, w):
    X, W_ = x.astype(np.float64), w.astype(np.float64)
    g = np.concatenate(list(X), axis=1)
    p = np.pad(g, ((0, 0), (H, H)))
    y = np.zeros((N, 128, W))
    for r in range(N):
        for i in range(KW):
            y[r] += W_[r][:, 128 * i:128 * i + 128].T @ p[:, W * r + i * DIL:W * r + i * DIL + W]
    return {"y": y.astype(ml_dtypes.bfloat16 if x.dtype != np.float64 else np.float64)}

from concourse.bass import DstId, RemoteDMATransfer

W, KW, DIL = 1024, 3, 4
H = (KW // 2) * DIL
C = 128
BANK = 512
NCH = 4
OUT = [H, 260, 516, 772, W - H]
PIECE = [0] + [b + H for b in OUT[1:]]
SLOT = 256
NE = 4

SCRATCH = {
    "xs":   ("sbuf", [C, W], "bfloat16"),
    "ws":   ("sbuf", [C, KW * C], "bfloat16"),
    "edge": ("sbuf", [C, 2 * H], "bfloat16"),
    "halo": ("sbuf", [C, 16], "bfloat16"),
    "ys":   ("sbuf", [C, NCH * SLOT], "bfloat16"),
    "ye":   ("sbuf", [C, 16], "bfloat16"),
    "ps":   ("psum", [C, (NCH + 2) * BANK], "float32"),
}
SEMAPHORES = (["e_ld", "w_ld", "halo_l", "halo_r", "sent", "mm_l", "mm_r", "cp_l", "cp_r", "st"]
              + ["x_ld%d" % k for k in range(NCH)] + ["mm%d" % k for k in range(NCH)] + ["cp%d" % k for k in range(NCH)])


def _pick(mask, n):
    out, b = 0, 0
    while n:
        if (mask >> b) & 1:
            out |= 1 << b
            n -= 1
        b += 1
    return out


def rank_program(g, core, T, topo):
    rank = T.rank_of(core)
    if rank is None:
        return
    S = T.sem
    left = T.cores[rank - 1] if rank > 0 else None
    right = T.cores[rank + 1] if rank + 1 < len(T.cores) else None
    tap = [T.ws[:, C * i:C * (i + 1)] for i in range(KW)]
    queue = [g.sync, g.scalar]

    n_edge = 0
    if left is not None:
        g.sync.dma_start(T.edge[:, 0:H], T.x[:, 0:H]).then_inc(S.e_ld, 16)
        n_edge += 16
    if right is not None:
        g.scalar.dma_start(T.edge[:, H:2 * H], T.x[:, W - H:W]).then_inc(S.e_ld, 16)
        n_edge += 16
    g.scalar.dma_start(T.ws[:], T.w[:]).then_inc(S.w_ld, 16)
    for k in range(NCH):
        a, b = PIECE[k], PIECE[k + 1]
        queue[k % 2].dma_start(T.xs[:, a:b], T.x[:, a:b]).then_inc(S["x_ld%d" % k], 16)

    sends = []
    if left is not None:
        sends.append((left, T.edge[:, 0:H], T.halo[:, 8:8 + H], S.halo_r))
    if right is not None:
        sends.append((right, T.edge[:, H:2 * H], T.halo[:, 0:H], S.halo_l))
    g.wait_ge(S.e_ld, n_edge)
    transfers, taken = [], 0
    for dst, src_ap, dst_ap, sem in sends:
        assert topo.may_write(core, dst)
        rid, pid = topo.addr(dst, core)
        m = _pick(topo.mask(core, dst) & ~taken, NE)
        taken |= m
        transfers.append(RemoteDMATransfer(dst_ids=[DstId(rid=rid, pnc=pid)], dma_engine_mask=m, remote_sem=sem,
                                           src=src_ap, dst=dst_ap))
    g.remote_dma_fused(transfers, local_sem=S.sent)

    te = g.tensor
    te.wait_ge(S.w_ld, 16)
    for k in range(NCH):
        a, b = OUT[k], OUT[k + 1]
        out = T.ps[:, BANK * k:BANK * k + (b - a)]
        te.wait_ge(S["x_ld%d" % k], 16)
        te.matmul(out, tap[1], T.xs[:, a:b], True, False)
        te.matmul(out, tap[0], T.xs[:, a - H:b - H], False, False)
        te.matmul(out, tap[2], T.xs[:, a + H:b + H], False, True).then_inc(S["mm%d" % k], 1)
    pl = T.ps[:, BANK * NCH:BANK * NCH + H]
    pr = T.ps[:, BANK * (NCH + 1):BANK * (NCH + 1) + H]
    te.matmul(pl, tap[1], T.xs[:, 0:H], True, False)
    if left is None:
        te.matmul(pl, tap[2], T.xs[:, H:2 * H], False, True).then_inc(S.mm_l, 1)
    else:
        te.matmul(pl, tap[2], T.xs[:, H:2 * H], False, False)
    te.matmul(pr, tap[1], T.xs[:, W - H:W], True, False)
    if right is None:
        te.matmul(pr, tap[0], T.xs[:, W - 2 * H:W - H], False, True).then_inc(S.mm_r, 1)
    else:
        te.matmul(pr, tap[0], T.xs[:, W - 2 * H:W - H], False, False)
    if left is not None:
        te.wait_ge(S.halo_l, NE)
        te.matmul(pl, tap[0], T.halo[:, 0:H], False, True).then_inc(S.mm_l, 1)
    if right is not None:
        te.wait_ge(S.halo_r, NE)
        te.matmul(pr, tap[2], T.halo[:, 8:8 + H], False, True).then_inc(S.mm_r, 1)

    ve = g.vector
    for k in range(NCH):
        n = OUT[k + 1] - OUT[k]
        ve.wait_ge(S["mm%d" % k], 1)
        ve.tensor_copy(T.ys[:, SLOT * k:SLOT * k + n], T.ps[:, BANK * k:BANK * k + n]).then_inc(S["cp%d" % k], 1)
    ve.wait_ge(S.mm_l, 1)
    ve.tensor_copy(T.ye[:, 0:H], pl).then_inc(S.cp_l, 1)
    ve.wait_ge(S.mm_r, 1)
    ve.tensor_copy(T.ye[:, 8:8 + H], pr).then_inc(S.cp_r, 1)

    for k in range(NCH):
        a, b = OUT[k], OUT[k + 1]
        q = queue[k % 2]
        q.wait_ge(S["cp%d" % k], 1)
        q.dma_start(T.y[:, a:b], T.ys[:, SLOT * k:SLOT * k + (b - a)]).then_inc(S.st, 16)
    g.sync.wait_ge(S.cp_l, 1)
    g.sync.dma_start(T.y[:, 0:H], T.ye[:, 0:H]).then_inc(S.st, 16)
    g.scalar.wait_ge(S.cp_r, 1)
    g.scalar.dma_start(T.y[:, W - H:W], T.ye[:, 8:8 + H]).then_inc(S.st, 16)

    g.wait_ge(S.sent, NE * len(transfers))
    g.wait_ge(S.st, 16 * (NCH + 2))
